import numpy as np
CORES = [31,71,111]
N = 3
W, KW = 128, 5
H = KW // 2
def setup_inputs(rng):
    return {"x": rng.standard_normal((N, 128, W), dtype=np.float32), "t": rng.standard_normal((N, 128, KW * W), dtype=np.float32)}
def setup_inputs_big(rng):
    d = setup_inputs(rng)
    for k in ("x", "t"): d[k] = (d[k].astype(np.float32) * 1024.0).astype(d[k].dtype)
    return d
def setup_inputs_small(rng):
    d = setup_inputs(rng)
    for k in ("x", "t"): d[k] = (d[k].astype(np.float32) * (1 / 1024.0)).astype(d[k].dtype)
    return d
def setup_inputs_apart(rng):
    d = setup_inputs(rng)
    f = (10.0 ** rng.permutation(np.linspace(-1.5, 1.5, N))).astype(np.float32).reshape(N, 1, 1)
    for k in ("x", "t"): d[k] = (d[k].astype(np.float32) * f).astype(d[k].dtype)
    return d
def reference(x, t):
    X, T = x.astype(np.float64), t.astype(np.float64)
    g = np.concatenate(list(X), axis=1)
    p = np.concatenate([g[:, -H:], g, g[:, :H]], axis=1)
    y = np.stack([sum(T[r][:, W * i:W * i + W] * p[:, W * r + i:W * r + i + W] for i in range(KW)) for r in range(N)])
    return {"y": y.astype(np.float32 if x.dtype != np.float64 else np.float64)}

@@ -1,0 +1,107 @@
+from concourse.bass import DstId, RemoteDMATransfer
+from concourse.mybir import AluOpType
+
+P, W, KW = 128, 128, 5
+H = KW // 2
+ENG = 4
+SPLIT = 3
+ROT = (KW - SPLIT) * W
+
+SCRATCH = {
+    "xs": ("sbuf", [P, W], "float32"),
+    "ts": ("sbuf", [P, KW * W], "float32"),
+    "halo": ("sbuf", [P, 2 * H], "float32"),
+    "xp": ("psum", [P, 512], "float32"),
+    "ac": ("psum", [P, 512], "float32"),
+    "pr": ("sbuf", [P, (KW - 1) * W], "float32"),
+    "pa": ("sbuf", [P, 2 * H], "float32"),
+    "pb": ("sbuf", [P, 2], "float32"),
+    "ys": ("sbuf", [P, W], "float32"),
+}
+SEMAPHORES = ["xl", "ta", "tb", "sent", "arr", "v", "st"]
+
+
+def _engines(mask, n, skip):
+    bits = [b for b in range(mask.bit_length()) if (mask >> b) & 1]
+    out = 0
+    for b in bits[skip:skip + n]:
+        out |= 1 << b
+    return out
+
+
+def rank_program(g, core, T, topo):
+    rank = T.rank_of(core)
+    if rank is None:
+        return
+    n = len(T.cores)
+    left, right = T.cores[(rank - 1) % n], T.cores[(rank + 1) % n]
+    S, V = T.sem, g.vector
+    mult, add = AluOpType.mult, AluOpType.add
+
+    g.sync.dma_start(T.xs[:], T.x[:]).then_inc(S.xl, 16)
+    g.sync.dma_start(T.ts[:, ROT:KW * W], T.t[:, 0:SPLIT * W]).then_inc(S.ta, 16)
+    g.sync.dma_start(T.ts[:, 0:ROT], T.t[:, SPLIT * W:KW * W]).then_inc(S.tb, 16)
+
+    assert topo.may_write(core, left) and topo.may_write(core, right)
+    both = topo.mask(core, left) & topo.mask(core, right)
+
+    def transfer(dst_core, src, dst, skip):
+        rid, pid, _ = topo.addr(dst_core)
+        return RemoteDMATransfer(dst_ids=[DstId(rid=rid, pnc=pid)], dma_engine_mask=_engines(both, ENG, skip),
+                                 remote_sem=S.arr, src=src, dst=dst)
+
+    g.wait_ge(S.xl, 16)
+    g.remote_dma_fused([transfer(right, T.xs[:, W - H:W], T.halo[:, H:2 * H], 0),
+                        transfer(left, T.xs[:, 0:H], T.halo[:, 0:H], ENG)], local_sem=S.sent)
+    g.wait_ge(S.sent, 2 * ENG)
+
+    nv = [0]
+
+    def did(ins):
+        ins.then_inc(S.v, 1)
+        nv[0] += 1
+
+    def settle():
+        V.wait_ge(S.v, nv[0])
+
+    def tab(i):
+        o = ROT + W * i if i < SPLIT else W * (i - SPLIT)
+        return T.ts[:, o:o + W]
+
+    def prod(i):
+        return T.pr[:, W * (i - 1):W * i]
+
+    acc = T.ac[:, 0:W]
+    did(V.memset(T.xp[:, 0:H], 0.0))
+    did(V.memset(T.xp[:, H + W:2 * H + W], 0.0))
+    V.wait_ge(S.xl, 16)
+    did(V.tensor_copy(T.xp[:, H:H + W], T.xs[:]))
+
+    V.wait_ge(S.ta, 16)
+    settle()
+    did(V.tensor_tensor(acc, tab(0), T.xp[:, 0:W], mult))
+    for i in range(1, SPLIT):
+        did(V.tensor_tensor(prod(i), tab(i), T.xp[:, i:i + W], mult))
+    for i in range(1, SPLIT):
+        settle()
+        did(V.tensor_tensor(acc, acc, prod(i), add))
+
+    V.wait_ge(S.tb, 16)
+    for i in range(SPLIT, KW):
+        did(V.tensor_tensor(prod(i), tab(i), T.xp[:, i:i + W], mult))
+    for i in range(SPLIT, KW):
+        settle()
+        did(V.tensor_tensor(T.ys[:] if i == KW - 1 else acc, acc, prod(i), add))
+
+    V.wait_ge(S.arr, 2 * ENG)
+    did(V.tensor_tensor(T.pa[:], T.halo[:], T.ts[:, ROT - H:ROT + H], mult))
+    did(V.tensor_tensor(T.pb[:], T.halo[:, 0:2 * H:2 * H - 1], T.ts[:, ROT - W - 1:ROT + W + 1:2 * W + 1], mult))
+    settle()
+    did(V.tensor_tensor(T.pa[:, 1:3], T.pa[:, 1:3], T.pb[:], add))
+    settle()
+    did(V.tensor_tensor(T.ys[:, W - H:W], T.ys[:, W - H:W], T.pa[:, 0:H], add))
+    did(V.tensor_tensor(T.ys[:, 0:H], T.ys[:, 0:H], T.pa[:, H:2 * H], add))
+
+    g.scalar.wait_ge(S.v, nv[0])
+    g.scalar.dma_start(T.y[:], T.ys[:]).then_inc(S.st, 16)
+    g.scalar.wait_ge(S.st, 16)

@@ -1,32 +1,32 @@
-from concourse.bass import DstId, RemoteDMATransfer
-from concourse.mybir import AluOpType
+from concourse.mybir import AluOpType, ActivationFunctionType
 
 P, W, KW = 128, 128, 5
 H = KW // 2
-ENG = 4
 SPLIT = 3
-ROT = (KW - SPLIT) * W
+HALF = W // 2
 
 SCRATCH = {
     "xs": ("sbuf", [P, W], "float32"),
     "ts": ("sbuf", [P, KW * W], "float32"),
-    "halo": ("sbuf", [P, 2 * H], "float32"),
+    "hl": ("sbuf", [P, H], "float32"),
+    "hr": ("sbuf", [P, H], "float32"),
     "xp": ("psum", [P, 512], "float32"),
     "ac": ("psum", [P, 512], "float32"),
     "pr": ("sbuf", [P, (KW - 1) * W], "float32"),
-    "pa": ("sbuf", [P, 2 * H], "float32"),
-    "pb": ("sbuf", [P, 2], "float32"),
     "ys": ("sbuf", [P, W], "float32"),
+    "tl": ("sbuf", [P, 1], "float32"),
+    "tr": ("sbuf", [P, 1], "float32"),
+    "el": ("sbuf", [P, H], "float32"),
+    "er": ("sbuf", [P, H], "float32"),
 }
-SEMAPHORES = ["xl", "ta", "tb", "sent", "arr", "v", "st"]
+SEMAPHORES = (["xl", "ta", "tb", "sent", "al", "ar", "z", "cp", "si", "sl", "sr"]
+              + ["m%d" % i for i in range(KW)]
+              + ["a%d%s" % (i, h) for i in range(1, KW) for h in "LR"]
+              + ["l1", "l2", "l3", "r1", "r2", "r3"])
 
 
-def _engines(mask, n, skip):
-    bits = [b for b in range(mask.bit_length()) if (mask >> b) & 1]
-    out = 0
-    for b in bits[skip:skip + n]:
-        out |= 1 << b
-    return out
+def _count(mask):
+    return bin(mask).count("1")
 
 
 def rank_program(g, core, T, topo):
@@ -35,73 +35,98 @@ def rank_program(g, core, T, topo):
         return
     n = len(T.cores)
     left, right = T.cores[(rank - 1) % n], T.cores[(rank + 1) % n]
-    S, V = T.sem, g.vector
+    S, V, A = T.sem, g.vector, g.scalar
     mult, add = AluOpType.mult, AluOpType.add
+    ident = ActivationFunctionType.Identity
 
     g.sync.dma_start(T.xs[:], T.x[:]).then_inc(S.xl, 16)
-    g.sync.dma_start(T.ts[:, ROT:KW * W], T.t[:, 0:SPLIT * W]).then_inc(S.ta, 16)
-    g.sync.dma_start(T.ts[:, 0:ROT], T.t[:, SPLIT * W:KW * W]).then_inc(S.tb, 16)
+    g.sync.dma_start(T.ts[:, 0:SPLIT * W], T.t[:, 0:SPLIT * W]).then_inc(S.ta, 16)
+    g.sync.dma_start(T.ts[:, SPLIT * W:KW * W], T.t[:, SPLIT * W:KW * W]).then_inc(S.tb, 16)
 
-    assert topo.may_write(core, left) and topo.may_write(core, right)
-    both = topo.mask(core, left) & topo.mask(core, right)
-
-    def transfer(dst_core, src, dst, skip):
+    def send(dst_core, src, dst, sem):
+        assert topo.may_write(core, dst_core)
         rid, pid, _ = topo.addr(dst_core)
-        return RemoteDMATransfer(dst_ids=[DstId(rid=rid, pnc=pid)], dma_engine_mask=_engines(both, ENG, skip),
-                                 remote_sem=S.arr, src=src, dst=dst)
+        m = topo.mask(core, dst_core)
+        g.remote_dma(out_ap=dst, in_ap=src, remote_sem=sem, local_sem=S.sent, pid=pid, routing_id=rid,
+                     dma_engine_mask=m)
+        return _count(m)
 
     g.wait_ge(S.xl, 16)
-    g.remote_dma_fused([transfer(right, T.xs[:, W - H:W], T.halo[:, H:2 * H], 0),
-                        transfer(left, T.xs[:, 0:H], T.halo[:, 0:H], ENG)], local_sem=S.sent)
-    g.wait_ge(S.sent, 2 * ENG)
-
-    nv = [0]
-
-    def did(ins):
-        ins.then_inc(S.v, 1)
-        nv[0] += 1
-
-    def settle():
-        V.wait_ge(S.v, nv[0])
+    left_us = send(right, T.xs[:, W - H:W], T.hl[:], S.al)
+    left_us += send(left, T.xs[:, 0:H], T.hr[:], S.ar)
+    g.wait_ge(S.sent, left_us)
 
     def tab(i):
-        o = ROT + W * i if i < SPLIT else W * (i - SPLIT)
-        return T.ts[:, o:o + W]
+        return T.ts[:, W * i:W * i + W]
 
-    def prod(i):
-        return T.pr[:, W * (i - 1):W * i]
+    def tcol(i, c):
+        return T.ts[:, W * i + c:W * i + c + 1]
 
-    acc = T.ac[:, 0:W]
-    did(V.memset(T.xp[:, 0:H], 0.0))
-    did(V.memset(T.xp[:, H + W:2 * H + W], 0.0))
+    def prod(i, lo=0, hi=W):
+        return T.pr[:, W * (i - 1) + lo:W * (i - 1) + hi]
+
+    def vwait(*names):
+        for nm in names:
+            V.wait_ge(S[nm], 1)
+
+    V.memset(T.xp[:, 0:H], 0.0).then_inc(S.z, 1)
+    V.memset(T.xp[:, H + W:2 * H + W], 0.0).then_inc(S.z, 1)
     V.wait_ge(S.xl, 16)
-    did(V.tensor_copy(T.xp[:, H:H + W], T.xs[:]))
+    V.tensor_copy(T.xp[:, H:H + W], T.xs[:]).then_inc(S.cp, 1)
+
+    halves = (("L", 0, HALF), ("R", HALF, W))
+
+    def sums(i, out=None):
+        for h, lo, hi in halves:
+            if i > 1:
+                vwait("a%d%s" % (i - 1, h))
+            dst = T.ac[:, lo:hi] if out is None else out[:, lo:hi]
+            V.tensor_tensor(dst, T.ac[:, lo:hi], prod(i, lo, hi), add).then_inc(S["a%d%s" % (i, h)], 1)
 
     V.wait_ge(S.ta, 16)
-    settle()
-    did(V.tensor_tensor(acc, tab(0), T.xp[:, 0:W], mult))
+    V.wait_ge(S.z, 2)
+    vwait("cp")
+    V.tensor_tensor(T.ac[:, 0:W], tab(0), T.xp[:, 0:W], mult).then_inc(S.m0, 1)
     for i in range(1, SPLIT):
-        did(V.tensor_tensor(prod(i), tab(i), T.xp[:, i:i + W], mult))
+        V.tensor_tensor(prod(i), tab(i), T.xp[:, i:i + W], mult).then_inc(S["m%d" % i], 1)
+    vwait("m0")
     for i in range(1, SPLIT):
-        settle()
-        did(V.tensor_tensor(acc, acc, prod(i), add))
+        vwait("m%d" % i)
+        sums(i)
 
     V.wait_ge(S.tb, 16)
     for i in range(SPLIT, KW):
-        did(V.tensor_tensor(prod(i), tab(i), T.xp[:, i:i + W], mult))
+        V.tensor_tensor(prod(i), tab(i), T.xp[:, i:i + W], mult).then_inc(S["m%d" % i], 1)
     for i in range(SPLIT, KW):
-        settle()
-        did(V.tensor_tensor(T.ys[:] if i == KW - 1 else acc, acc, prod(i), add))
+        vwait("m%d" % i)
+        sums(i, T.ys if i == KW - 1 else None)
+    lastL, lastR = "a%dL" % (KW - 1), "a%dR" % (KW - 1)
 
-    V.wait_ge(S.arr, 2 * ENG)
-    did(V.tensor_tensor(T.pa[:], T.halo[:], T.ts[:, ROT - H:ROT + H], mult))
-    did(V.tensor_tensor(T.pb[:], T.halo[:, 0:2 * H:2 * H - 1], T.ts[:, ROT - W - 1:ROT + W + 1:2 * W + 1], mult))
-    settle()
-    did(V.tensor_tensor(T.pa[:, 1:3], T.pa[:, 1:3], T.pb[:], add))
-    settle()
-    did(V.tensor_tensor(T.ys[:, W - H:W], T.ys[:, W - H:W], T.pa[:, 0:H], add))
-    did(V.tensor_tensor(T.ys[:, 0:H], T.ys[:, 0:H], T.pa[:, H:2 * H], add))
+    vwait(lastL)
+    V.wait_ge(S.al, _count(topo.mask(left, core)))
+    V.tensor_scalar(T.tl[:], T.hl[:, 1:2], tcol(1, 0), T.ys[:, 0:1], mult, add).then_inc(S.l1, 1)
+    V.tensor_scalar(T.el[:, 1:2], T.hl[:, 1:2], tcol(0, 1), T.ys[:, 1:2], mult, add).then_inc(S.l2, 1)
+    vwait("l1")
+    V.tensor_scalar(T.el[:, 0:1], T.hl[:, 0:1], tcol(0, 0), T.tl[:], mult, add).then_inc(S.l3, 1)
 
-    g.scalar.wait_ge(S.v, nv[0])
-    g.scalar.dma_start(T.y[:], T.ys[:]).then_inc(S.st, 16)
-    g.scalar.wait_ge(S.st, 16)
+    A.wait_ge(S.tb, 16)
+    A.wait_ge(S[lastR], 1)
+    A.wait_ge(S.ar, _count(topo.mask(right, core)))
+    A.activation(T.tr[:], T.hr[:, 0:1], ident, bias=T.ys[:, W - 1:W], scale=tcol(3, W - 1)).then_inc(S.r1, 1)
+    A.activation(T.er[:, 0:1], T.hr[:, 0:1], ident, bias=T.ys[:, W - 2:W - 1],
+                 scale=tcol(4, W - 2)).then_inc(S.r2, 1)
+    A.wait_ge(S.r1, 1)
+    A.activation(T.er[:, 1:2], T.hr[:, 1:2], ident, bias=T.tr[:], scale=tcol(4, W - 1)).then_inc(S.r3, 1)
+    A.wait_ge(S.r2, 1)
+    A.wait_ge(S.r3, 1)
+    A.dma_start(T.y[:, W - H:W], T.er[:]).then_inc(S.sr, 16)
+    A.wait_ge(S.sr, 16)
+
+    g.sync.wait_ge(S[lastL], 1)
+    g.sync.wait_ge(S[lastR], 1)
+    g.sync.dma_start(T.y[:, H:W - H], T.ys[:, H:W - H]).then_inc(S.si, 16)
+    g.sync.wait_ge(S.l2, 1)
+    g.sync.wait_ge(S.l3, 1)
+    g.sync.dma_start(T.y[:, 0:H], T.el[:]).then_inc(S.sl, 16)
+    g.sync.wait_ge(S.si, 16)
+    g.sync.wait_ge(S.sl, 16)

from concourse.mybir import AluOpType, ActivationFunctionType

P, W, KW = 128, 128, 5
H = KW // 2
SPLIT = 3
HALF = W // 2

SCRATCH = {
    "xs": ("sbuf", [P, W], "float32"),
    "ts": ("sbuf", [P, KW * W], "float32"),
    "hl": ("sbuf", [P, H], "float32"),
    "hr": ("sbuf", [P, H], "float32"),
    "xp": ("psum", [P, 512], "float32"),
    "ac": ("psum", [P, 512], "float32"),
    "pr": ("sbuf", [P, (KW - 1) * W], "float32"),
    "ys": ("sbuf", [P, W], "float32"),
    "tl": ("sbuf", [P, 1], "float32"),
    "tr": ("sbuf", [P, 1], "float32"),
    "el": ("sbuf", [P, H], "float32"),
    "er": ("sbuf", [P, H], "float32"),
}
SEMAPHORES = (["xl", "ta", "tb", "sent", "al", "ar", "z", "cp", "si", "sl", "sr"]
              + ["m%d" % i for i in range(KW)]
              + ["a%d%s" % (i, h) for i in range(1, KW) for h in "LR"]
              + ["l1", "l2", "l3", "r1", "r2", "r3"])


def _count(mask):
    return bin(mask).count("1")


def rank_program(g, core, T, topo):
    rank = T.rank_of(core)
    if rank is None:
        return
    n = len(T.cores)
    left, right = T.cores[(rank - 1) % n], T.cores[(rank + 1) % n]
    S, V, A = T.sem, g.vector, g.scalar
    mult, add = AluOpType.mult, AluOpType.add
    ident = ActivationFunctionType.Identity

    g.sync.dma_start(T.xs[:], T.x[:]).then_inc(S.xl, 16)
    g.sync.dma_start(T.ts[:, 0:SPLIT * W], T.t[:, 0:SPLIT * W]).then_inc(S.ta, 16)
    g.sync.dma_start(T.ts[:, SPLIT * W:KW * W], T.t[:, SPLIT * W:KW * W]).then_inc(S.tb, 16)

    def send(dst_core, src, dst, sem):
        assert topo.may_write(core, dst_core)
        rid, pid, _ = topo.addr(dst_core)
        m = topo.mask(core, dst_core)
        g.remote_dma(out_ap=dst, in_ap=src, remote_sem=sem, local_sem=S.sent, pid=pid, routing_id=rid,
                     dma_engine_mask=m)
        return _count(m)

    g.wait_ge(S.xl, 16)
    left_us = send(right, T.xs[:, W - H:W], T.hl[:], S.al)
    left_us += send(left, T.xs[:, 0:H], T.hr[:], S.ar)
    g.wait_ge(S.sent, left_us)

    def tab(i):
        return T.ts[:, W * i:W * i + W]

    def tcol(i, c):
        return T.ts[:, W * i + c:W * i + c + 1]

    def prod(i, lo=0, hi=W):
        return T.pr[:, W * (i - 1) + lo:W * (i - 1) + hi]

    def vwait(*names):
        for nm in names:
            V.wait_ge(S[nm], 1)

    V.memset(T.xp[:, 0:H], 0.0).then_inc(S.z, 1)
    V.memset(T.xp[:, H + W:2 * H + W], 0.0).then_inc(S.z, 1)
    V.wait_ge(S.xl, 16)
    V.tensor_copy(T.xp[:, H:H + W], T.xs[:]).then_inc(S.cp, 1)

    halves = (("L", 0, HALF), ("R", HALF, W))

    def sums(i, out=None):
        for h, lo, hi in halves:
            if i > 1:
                vwait("a%d%s" % (i - 1, h))
            dst = T.ac[:, lo:hi] if out is None else out[:, lo:hi]
            V.tensor_tensor(dst, T.ac[:, lo:hi], prod(i, lo, hi), add).then_inc(S["a%d%s" % (i, h)], 1)

    V.wait_ge(S.ta, 16)
    V.wait_ge(S.z, 2)
    vwait("cp")
    V.tensor_tensor(T.ac[:, 0:W], tab(0), T.xp[:, 0:W], mult).then_inc(S.m0, 1)
    for i in range(1, SPLIT):
        V.tensor_tensor(prod(i), tab(i), T.xp[:, i:i + W], mult).then_inc(S["m%d" % i], 1)
    vwait("m0")
    for i in range(1, SPLIT):
        vwait("m%d" % i)
        sums(i)

    V.wait_ge(S.tb, 16)
    for i in range(SPLIT, KW):
        V.tensor_tensor(prod(i), tab(i), T.xp[:, i:i + W], mult).then_inc(S["m%d" % i], 1)
    for i in range(SPLIT, KW):
        vwait("m%d" % i)
        sums(i, T.ys if i == KW - 1 else None)
    lastL, lastR = "a%dL" % (KW - 1), "a%dR" % (KW - 1)

    vwait(lastL)
    V.wait_ge(S.al, _count(topo.mask(left, core)))
    V.tensor_scalar(T.tl[:], T.hl[:, 1:2], tcol(1, 0), T.ys[:, 0:1], mult, add).then_inc(S.l1, 1)
    V.tensor_scalar(T.el[:, 1:2], T.hl[:, 1:2], tcol(0, 1), T.ys[:, 1:2], mult, add).then_inc(S.l2, 1)
    vwait("l1")
    V.tensor_scalar(T.el[:, 0:1], T.hl[:, 0:1], tcol(0, 0), T.tl[:], mult, add).then_inc(S.l3, 1)

    A.wait_ge(S.tb, 16)
    A.wait_ge(S[lastR], 1)
    A.wait_ge(S.ar, _count(topo.mask(right, core)))
    A.activation(T.tr[:], T.hr[:, 0:1], ident, bias=T.ys[:, W - 1:W], scale=tcol(3, W - 1)).then_inc(S.r1, 1)
    A.activation(T.er[:, 0:1], T.hr[:, 0:1], ident, bias=T.ys[:, W - 2:W - 1],
                 scale=tcol(4, W - 2)).then_inc(S.r2, 1)
    A.wait_ge(S.r1, 1)
    A.activation(T.er[:, 1:2], T.hr[:, 1:2], ident, bias=T.tr[:], scale=tcol(4, W - 1)).then_inc(S.r3, 1)
    A.wait_ge(S.r2, 1)
    A.wait_ge(S.r3, 1)
    A.dma_start(T.y[:, W - H:W], T.er[:]).then_inc(S.sr, 16)
    A.wait_ge(S.sr, 16)

    g.sync.wait_ge(S[lastL], 1)
    g.sync.wait_ge(S[lastR], 1)
    g.sync.dma_start(T.y[:, H:W - H], T.ys[:, H:W - H]).then_inc(S.si, 16)
    g.sync.wait_ge(S.l2, 1)
    g.sync.wait_ge(S.l3, 1)
    g.sync.dma_start(T.y[:, 0:H], T.el[:]).then_inc(S.sl, 16)
    g.sync.wait_ge(S.si, 16)
    g.sync.wait_ge(S.sl, 16)
